import numpy as np
import ml_dtypes


def mxq(x, axis, fmt="e4m3"):
    dtype, down = {"e4m3": (ml_dtypes.float8_e4m3fn, 7), "e5m2": (ml_dtypes.float8_e5m2, 14)}[fmt]
    v = np.moveaxis(np.asarray(x, np.float32).astype(ml_dtypes.bfloat16).astype(np.float64), axis, -1)
    blocks = v.reshape(v.shape[:-1] + (-1, 32))
    amax = np.abs(blocks).max(-1, keepdims=True)
    byte = np.maximum(np.where(amax > 0, np.frexp(amax)[1] - 1 + 127, 0) - down, 1)
    scale = np.exp2(byte - 127.0)
    codes = (blocks / scale).astype(np.float32).astype(dtype).astype(np.float64)
    return np.moveaxis((codes * scale).reshape(v.shape), -1, axis)


WIDE = False


def mx_kscale(k):
    if not WIDE:
        return np.ones(k)
    levels = np.array([10, -10, 5, -5, 0])
    if k % 512:
        return np.exp2(np.random.permutation(np.resize(levels, k // 32))).repeat(32)
    a = np.empty((k // 512, 16))
    for p in range(k // 512):
        a[p, :8] = np.random.permutation(np.resize(levels, 8))
        for g in range(8):
            far = levels[np.abs(levels - a[p, g]) >= 10]
            a[p, g + 8] = far[np.random.randint(len(far))]
    return np.exp2(a.ravel()).repeat(32)


def f64(x):
    return np.asarray(x).astype(np.float64)


def striped(idx):
    return np.tile(np.asarray(idx).reshape(-1, 16).T, (8, 1)).astype(np.uint16)


def unstriped(offs):
    return offs[:16].T.reshape(-1).astype(np.int64)


E2M1 = np.array([0.0, 0.5, 1.0, 1.5, 2.0, 3.0, 4.0, 6.0, -0.0, -0.5, -1.0, -1.5, -2.0, -3.0, -4.0, -6.0])


def pack_weight(w, fmt):
    k, n = w.shape
    w = f64(np.asarray(w, np.float32).astype(ml_dtypes.bfloat16)).reshape(k // 32, 32, n)
    amax = np.abs(w).max(1)
    if fmt == "e4m3":
        byte = np.frexp(amax)[1] - 1 + 127 - 7
    else:
        mant, ex = np.frexp(amax / 6.0)
        byte = np.where(mant > 0.5, ex, ex - 1) + 127
    byte = np.clip(np.where(amax > 0, byte, 1), 1, 254)
    scaled = (w * np.exp2(127.0 - byte)[:, None, :]).reshape(k, n).astype(np.float32)
    by_word = np.ascontiguousarray(scaled.reshape(k // 512, 128, 4, n).transpose(0, 1, 3, 2))
    if fmt == "e4m3":
        words = by_word.astype(ml_dtypes.float8_e4m3fn).view(np.uint8)
    else:
        c = by_word.astype(ml_dtypes.float4_e2m1fn).view(np.uint8) & 0xF
        words = (c[..., 0::2] | (c[..., 1::2] << 4)).reshape(k // 512, 128, 2 * n)
    return np.ascontiguousarray(words), np.ascontiguousarray(byte.astype(np.uint8).reshape(k // 512, 16, n))


def unpack_weight(words, scales, fmt):
    g, _, n = scales.shape
    words = np.ascontiguousarray(words).reshape(g, 128, n, -1)
    if fmt == "e4m3":
        vals = words.view(ml_dtypes.float8_e4m3fn).astype(np.float64)
    else:
        nib = np.empty((g, 128, n, 4), np.uint8)
        nib[..., 0::2] = words & 0xF
        nib[..., 1::2] = words >> 4
        vals = E2M1[nib]
    vals = vals * np.repeat(np.exp2(scales.astype(np.float64) - 127.0), 8, axis=1)[..., None]
    return vals.transpose(0, 1, 3, 2).reshape(g * 512, n)


def bf(x):
    return np.asarray(x, np.float32).astype(ml_dtypes.bfloat16)


def planes(Y):
    r, m = Y.shape
    b = f64(bf(Y)).reshape(r // 32, 32, m)
    amax = np.abs(b).max(1)
    byte = np.clip(np.where(amax > 0, np.frexp(amax)[1] - 1 + 127 - 7, 1), 1, 254)
    codes = (b * np.exp2(127.0 - byte)[:, None, :]).reshape(r, m).astype(np.float32).astype(ml_dtypes.float8_e4m3fn).view(np.uint8)
    words = codes.reshape(r // 512, 128, 4, m).transpose(0, 1, 3, 2)
    return np.ascontiguousarray(words), np.ascontiguousarray(byte.astype(np.uint8).reshape(r // 512, 16, m))


D, T, I, Q, E = 512, 2048, 512, 256, 512


def setup_inputs():
    n = np.random.standard_normal
    idx = np.random.permutation(T)[:I]
    idx2 = np.random.permutation(T)[:I]
    fd = mx_kscale(D)
    fi = mx_kscale(I)
    keysp = pack_weight(n((D, T)) / fd[:, None], "e2m1")
    return {
        "query": (n((D, Q)) * 0.25 / np.sqrt(D) * fd[:, None]).astype(np.float32),
        "keys_words": keysp[0],
        "keys_scales": keysp[1],
        "size": (np.random.uniform(0.5, 2.0, (1, I)) * fi).astype(np.float32),
        "vsc": (np.random.uniform(0.5, 2.0, (I, 1)) / fi[:, None]).astype(np.float32),
        "vals": (n((E, T))).astype(np.float32),
        "svals": (n((E, T))).astype(np.float32),
        "offs": striped(idx),
        "offs2": striped(idx2),
    }


def reference(query, keys_words, keys_scales, size, vsc, vals, svals, offs, offs2):
    idx = unstriped(offs)
    idx2 = unstriped(offs2)
    keysu = unpack_weight(keys_words, keys_scales, "e2m1")
    queryq = mxq(f64(query), 0, "e4m3")
    keysidxg = keysu[:, idx]
    a = queryq.T @ keysidxg
    p = np.exp(a - np.max(a, axis=1, keepdims=True))
    w = p * f64(size) / np.sum(p, axis=1, keepdims=True)
    wt = w.T
    v1 = f64(vals)[:, idx2].T
    v2 = f64(svals)[:, idx].T
    vv = (v1 + np.tanh(v2)) * f64(vsc)
    vvq = mxq(vv, 0, "e4m3")
    wtq = mxq(wt, 0, "e4m3")
    o = vvq.T @ wtq
    words, scales = planes(o)
    return o, words, scales

@@ -1,0 +1,175 @@
+from contextlib import ExitStack
+
+import concourse.mybir as mybir
+from concourse.masks import make_identity
+
+D, T, I, Q, E = 512, 2048, 512, 256, 512
+FLOPS = 2 * Q * I * D + 2 * E * I * Q
+
+F32 = mybir.dt.float32
+BF16 = mybir.dt.bfloat16
+I32 = mybir.dt.int32
+U32 = mybir.dt.uint32
+U16 = mybir.dt.uint16
+U8 = mybir.dt.uint8
+FP8X4 = mybir.dt.float8_e4m3fn_x4
+FP4X4 = mybir.dt.float4_e2m1fn_x4
+ACT = mybir.ActivationFunctionType
+ALU = mybir.AluOpType
+
+P = 128
+PACK = 4
+HALVES = Q // P
+LIST_COLS = I // 16
+POOL_BYTES = 4 * T
+
+
+def tile_attend_keyhere_valuethere_pl_kernel(tc, query, keys_words, keys_scales, size, vsc, vals, svals, offs, offs2, out_0, out_1, out_2):
+    nc = tc.nc
+    with ExitStack() as ctx:
+        keep = ctx.enter_context(tc.tile_pool(name="keep", bufs=1))
+        psum = ctx.enter_context(tc.psum_pool(name="psum", bufs=1))
+
+        key_bytes = keep.tile([P, T], U8, name="key_bytes")
+        nc.vector.memset(key_bytes[:].bitcast(I32), 0)
+        ident = keep.tile([P, P], F32, name="ident")
+        make_identity(nc, ident[:])
+
+        key_words = keep.tile([P, T], U16, name="key_words")
+        list1 = keep.tile([P, LIST_COLS], U16, name="list1")
+        list2 = keep.tile([P, LIST_COLS], U16, name="list2")
+        q_raw = keep.tile([P, PACK, Q], F32, name="q_raw")
+        size_t = keep.tile([P, PACK], F32, name="size_t")
+        vsc_t = keep.tile([P, PACK], F32, name="vsc_t")
+        tokens = ctx.enter_context(tc.tile_pool(name="tokens", bufs=1))
+        s_at = [2 * j * POOL_BYTES for j in range(PACK)]
+        v_at = [(2 * j + 1) * POOL_BYTES for j in range(PACK)]
+        s_pool = [tokens.tile([P, T], F32, name="s_pool%d" % j, offset=s_at[j], align_bytes=64) for j in range(PACK)]
+        v_pool = [tokens.tile([P, T], F32, name="v_pool%d" % j, offset=v_at[j], align_bytes=64) for j in range(PACK)]
+        vals_dealt = vals.rearrange("(p j) t -> p j t", j=PACK)
+        svals_dealt = svals.rearrange("(p j) t -> p j t", j=PACK)
+
+        nc.sync.dma_start(out=key_words[:].bitcast(I32), in_=keys_words[0].bitcast(I32))
+        nc.sync.dma_start(list1[:], offs)
+        for g in range(4):
+            nc.sync.dma_start(out=key_bytes[32 * g : 32 * g + 4, :].bitcast(I32), in_=keys_scales[0, 4 * g : 4 * g + 4, :].bitcast(I32))
+        nc.sync.dma_start(out=q_raw[:], in_=query.rearrange("(p j) q -> p j q", j=PACK))
+        nc.sync.dma_start(out=s_pool[0][:], in_=svals_dealt[:, 0, :])
+        nc.sync.dma_start(list2[:], offs2)
+        nc.sync.dma_start(out=v_pool[0][:], in_=vals_dealt[:, 0, :])
+        nc.sync.dma_start(out=vsc_t[:], in_=vsc.rearrange("(p t) o -> p (t o)", t=PACK))
+        nc.sync.dma_start(out=size_t[:], in_=size.rearrange("o (p t) -> p (o t)", t=PACK))
+        for j in range(1, PACK):
+            nc.sync.dma_start(out=s_pool[j][:], in_=svals_dealt[:, j, :])
+            nc.sync.dma_start(out=v_pool[j][:], in_=vals_dealt[:, j, :])
+
+        k_codes = keep.tile([P, I], U16, name="k_codes", align_bytes=64)
+        k_scales = keep.tile([P, I], U8, name="k_scales", align_bytes=64)
+        q_bf = keep.tile([P, Q, PACK], BF16, name="q_bf", tag="s_got0", align_bytes=64)
+        q_codes = keep.tile([P, Q], U32, name="q_codes", align_bytes=64)
+        q_scales = keep.tile([P, Q], U8, name="q_scales", align_bytes=64)
+        w_bf = tokens.tile([P, Q, PACK], BF16, name="w_bf", offset=s_at[1] + 2048, align_bytes=64)
+        w_codes = tokens.tile([P, Q], U32, name="w_codes", offset=v_at[1] + 2048, align_bytes=64)
+        w_scales = keep.tile([P, Q], U8, name="w_scales", align_bytes=64)
+        neg_max = tokens.tile([P, HALVES], F32, name="neg_max", offset=s_at[0], align_bytes=64)
+        row_sum = keep.tile([P, HALVES], F32, name="row_sum")
+        inv_sum = tokens.tile([P, HALVES], F32, name="inv_sum", offset=v_at[0], align_bytes=64)
+        p_dealt = [keep.tile([P, PACK, P], F32, name="p_dealt%d" % h) for h in range(HALVES)]
+        p_norm = [keep.tile([P, PACK, P], F32, name="p_norm%d" % h) for h in range(HALVES)]
+        score = [psum.tile([P, I], F32, name="score%d" % h) for h in range(HALVES)]
+        p_turned = [psum.tile([P, PACK, P], F32, name="p_turned%d" % h) for h in range(HALVES)]
+        result = [psum.tile([P, PACK, P], F32, name="result%d" % h) for h in range(HALVES)]
+        o_f32 = keep.tile([P, PACK, Q], F32, name="o_f32")
+        o_bf = keep.tile([P, Q, PACK], BF16, name="o_bf", align_bytes=64)
+        o_codes = keep.tile([P, Q], U32, name="o_codes", align_bytes=64)
+        o_scales = keep.tile([P, Q], U8, name="o_scales", align_bytes=64)
+        out_dealt = out_0.rearrange("(p j) q -> p j q", j=PACK)
+        v_sum, v_bf, v_codes, v_scales = {}, {}, {}, {}
+
+        def half(h):
+            return slice(h * P, (h + 1) * P)
+
+        def quantise(codes, scales, source):
+            nc.vector.quantize_mx(out=codes.bitcast(FP8X4), scales=scales, in_=source.rearrange("p c t -> p (c t)"))
+
+        def gather_svals(j):
+            v_sum[j] = psum.tile([P, PACK, P], F32, name="v_sum", bufs=2)
+            s_got = keep.tile([P, I], F32, name="s_got%d" % j, align_bytes=64)
+            s_tanh = keep.tile([P, PACK, P], F32, name="s_tanh%d" % j)
+            nc.vector.tensor_copy(s_got[:], s_pool[j][:].indirect(list1[:]))
+            nc.scalar.activation(out=s_tanh[:].rearrange("p t s -> p s t"), in_=s_got[:].rearrange("p (s t) -> p s t", t=PACK), func=ACT.Tanh)
+            for t in range(PACK):
+                nc.tensor.matmul(v_sum[j][:, t, :], lhsT=s_tanh[:, t, :], rhs=ident[:], is_transpose=True, start=(t == 0), stop=False)
+
+        def gather_vals(j):
+            v_got = keep.tile([P, I], F32, name="v_got%d" % j)
+            nc.vector.tensor_copy(v_got[:], v_pool[j][:].indirect(list2[:]))
+            for t in range(PACK):
+                nc.tensor.matmul(v_sum[j][:, t, :], lhsT=v_got[:, t:I:PACK], rhs=ident[:], is_transpose=True, start=False, stop=(t == PACK - 1))
+
+        def scale_values(j):
+            v_bf[j] = tokens.tile([P, P, PACK], BF16, name="v_bf%d" % j, offset=s_at[(j + 1) % PACK] + 1024, align_bytes=64)
+            nc.vector.tensor_tensor(out=v_bf[j][:], in0=v_sum[j][:].rearrange("p t e -> p e t"),
+                                    in1=vsc_t[:].unsqueeze(1).broadcast_to([P, P, PACK]), op=ALU.mult)
+
+        def quantise_values(j):
+            v_codes[j] = tokens.tile([P, P], U32, name="v_codes%d" % j, offset=v_at[(j + 1) % PACK] + 1024, align_bytes=64)
+            v_scales[j] = keep.tile([P, P], U8, name="v_scales%d" % j, align_bytes=64)
+            quantise(v_codes[j][:], v_scales[j][:], v_bf[j][:])
+
+        def multiply(j):
+            for h in range(HALVES):
+                nc.tensor.matmul_mx(out=result[h][:, j, :], lhsT=v_codes[j][:].bitcast(FP8X4), lhsT_scale=v_scales[j][:],
+                                    rhs=w_codes[:, half(h)].bitcast(FP8X4), rhs_scale=w_scales[:, half(h)], start=True, stop=True)
+
+        def scale_weights(h):
+            nc.vector.tensor_tensor(out=w_bf[:, half(h), :], in0=p_turned[h][:].rearrange("p t q -> p q t"),
+                                    in1=size_t[:].unsqueeze(1).broadcast_to([P, P, PACK]), op=ALU.mult)
+
+        nc.vector.tensor_copy(k_codes[:], key_words[:].indirect(list1[:]))
+        nc.vector.tensor_copy(k_scales[:], key_bytes[:].indirect(list1[:]))
+        nc.scalar.copy(out=q_bf[:], in_=q_raw[:].rearrange("p j q -> p q j"))
+        quantise(q_codes[:], q_scales[:], q_bf[:])
+        for h in range(HALVES):
+            nc.tensor.matmul_mx(out=score[h][:], lhsT=q_codes[:, half(h)].bitcast(FP8X4), lhsT_scale=q_scales[:, half(h)],
+                                rhs=k_codes[:].bitcast(FP4X4), rhs_scale=k_scales[:], start=True, stop=True)
+        gather_svals(0)
+        for h in range(HALVES):
+            nc.vector.tensor_reduce(out=neg_max[:, h : h + 1], in_=score[h][:], axis=mybir.AxisListType.X, op=ALU.max, negate=True)
+            nc.scalar.activation(out=p_dealt[h][:].rearrange("p t s -> p s t"), in_=score[h][:].rearrange("p (s t) -> p s t", t=PACK),
+                                 func=ACT.Exp, bias=neg_max[:, h : h + 1], scale=1.0, accum_out=row_sum[:, h : h + 1])
+        gather_vals(0)
+        nc.vector.reciprocal(out=inv_sum[:], in_=row_sum[:])
+        for h in range(HALVES):
+            nc.scalar.activation(out=p_norm[h][:], in_=p_dealt[h][:], func=ACT.Copy, scale=inv_sum[:, h : h + 1])
+            for t in range(PACK):
+                nc.tensor.transpose(p_turned[h][:, t, :], p_norm[h][:, t, :], ident[:])
+        for j in range(1, PACK):
+            gather_svals(j)
+            scale_values(j - 1)
+            if j == 1:
+                scale_weights(0)
+                scale_weights(1)
+            gather_vals(j)
+            quantise_values(j - 1)
+            if j == 1:
+                quantise(w_codes[:], w_scales[:], w_bf[:])
+            multiply(j - 1)
+            for h in range(HALVES):
+                nc.scalar.copy(out=o_f32[:, j - 1, half(h)], in_=result[h][:, j - 1, :])
+        nc.sync.dma_start(out=out_dealt[:, 0 : PACK - 1, :], in_=o_f32[:, 0 : PACK - 1, :])
+        scale_values(PACK - 1)
+        quantise_values(PACK - 1)
+        multiply(PACK - 1)
+
+        nc.vector.tensor_copy(out=o_bf[:, half(0), :], in_=result[0][:].rearrange("p j q -> p q j"))
+        nc.scalar.copy(out=o_bf[:, half(1), :], in_=result[1][:].rearrange("p j q -> p q j"))
+        for h in (1, 0):
+            nc.scalar.copy(out=o_f32[:, PACK - 1, half(h)], in_=result[h][:, PACK - 1, :])
+        for h in (1, 0):
+            quantise(o_codes[:, half(h)], o_scales[:, half(h)], o_bf[:, half(h), :])
+        nc.scalar.dma_start(out=out_dealt[:, PACK - 1, :], in_=o_f32[:, PACK - 1, :])
+        nc.sync.dma_start(out=out_1[0].rearrange("p q r -> p (q r)").bitcast(I32), in_=o_codes[:].bitcast(I32))
+        for g in range(4):
+            queue = nc.sync if g < 2 else nc.scalar
+            queue.dma_start(out=out_2[0, 4 * g : 4 * g + 4, :].bitcast(I32), in_=o_scales[32 * g : 32 * g + 4, :].bitcast(I32))

@@ -68,8 +68,7 @@ def tile_attend_keyhere_valuethere_pl_kernel(tc, query, keys_words, keys_scales,
         q_bf = keep.tile([P, Q, PACK], BF16, name="q_bf", tag="s_got0", align_bytes=64)
         q_codes = keep.tile([P, Q], U32, name="q_codes", align_bytes=64)
         q_scales = keep.tile([P, Q], U8, name="q_scales", align_bytes=64)
-        w_bf = tokens.tile([P, Q, PACK], BF16, name="w_bf", offset=s_at[1] + 2048, align_bytes=64)
-        w_codes = tokens.tile([P, Q], U32, name="w_codes", offset=v_at[1] + 2048, align_bytes=64)
+        w_codes = tokens.tile([P, Q], U32, name="w_codes", offset=v_at[2], align_bytes=64)
         w_scales = keep.tile([P, Q], U8, name="w_scales", align_bytes=64)
         neg_max = tokens.tile([P, HALVES], F32, name="neg_max", offset=s_at[0], align_bytes=64)
         row_sum = keep.tile([P, HALVES], F32, name="row_sum")
@@ -102,10 +101,10 @@ def tile_attend_keyhere_valuethere_pl_kernel(tc, query, keys_words, keys_scales,
                 nc.tensor.matmul(v_sum[j][:, t, :], lhsT=s_tanh[:, t, :], rhs=ident[:], is_transpose=True, start=(t == 0), stop=False)
 
         def gather_vals(j):
-            v_got = keep.tile([P, I], F32, name="v_got%d" % j)
-            nc.vector.tensor_copy(v_got[:], v_pool[j][:].indirect(list2[:]))
+            v_got = keep.tile([P, PACK, P], F32, name="v_got%d" % j)
+            nc.vector.tensor_copy(v_got[:].bitcast(U32).rearrange("p t s -> p s t"), v_pool[j][:].bitcast(U32).indirect(list2[:]))
             for t in range(PACK):
-                nc.tensor.matmul(v_sum[j][:, t, :], lhsT=v_got[:, t:I:PACK], rhs=ident[:], is_transpose=True, start=False, stop=(t == PACK - 1))
+                nc.tensor.matmul(v_sum[j][:, t, :], lhsT=v_got[:, t, :], rhs=ident[:], is_transpose=True, start=False, stop=(t == PACK - 1))
 
         def scale_values(j):
             v_bf[j] = tokens.tile([P, P, PACK], BF16, name="v_bf%d" % j, offset=s_at[(j + 1) % PACK] + 1024, align_bytes=64)
@@ -122,9 +121,11 @@ def tile_attend_keyhere_valuethere_pl_kernel(tc, query, keys_words, keys_scales,
                 nc.tensor.matmul_mx(out=result[h][:, j, :], lhsT=v_codes[j][:].bitcast(FP8X4), lhsT_scale=v_scales[j][:],
                                     rhs=w_codes[:, half(h)].bitcast(FP8X4), rhs_scale=w_scales[:, half(h)], start=True, stop=True)
 
-        def scale_weights(h):
-            nc.vector.tensor_tensor(out=w_bf[:, half(h), :], in0=p_turned[h][:].rearrange("p t q -> p q t"),
-                                    in1=size_t[:].unsqueeze(1).broadcast_to([P, P, PACK]), op=ALU.mult)
+        def store_ready(first, last):
+            for j in range(first, last):
+                multiply(j)
+            for h in range(HALVES):
+                nc.scalar.copy(out=o_f32[:, first:last, half(h)], in_=result[h][:, first:last, :])
 
         nc.vector.tensor_copy(k_codes[:], key_words[:].indirect(list1[:]))
         nc.vector.tensor_copy(k_scales[:], key_bytes[:].indirect(list1[:]))
@@ -146,24 +147,28 @@ def tile_attend_keyhere_valuethere_pl_kernel(tc, query, keys_words, keys_scales,
                 nc.tensor.transpose(p_turned[h][:, t, :], p_norm[h][:, t, :], ident[:])
         for j in range(1, PACK):
             gather_svals(j)
-            scale_values(j - 1)
             if j == 1:
-                scale_weights(0)
-                scale_weights(1)
+                w_bf = keep.tile([P, Q, PACK], BF16, name="w_bf", tag="s_got1", align_bytes=64)
+                for h in range(HALVES):
+                    for t in range(PACK):
+                        nc.scalar.activation(out=w_bf[:, half(h), t], in_=p_turned[h][:, t, :], func=ACT.Copy, scale=size_t[:, t : t + 1])
+            scale_values(j - 1)
             gather_vals(j)
             quantise_values(j - 1)
-            if j == 1:
+            if j == 2:
                 quantise(w_codes[:], w_scales[:], w_bf[:])
-            multiply(j - 1)
-            for h in range(HALVES):
-                nc.scalar.copy(out=o_f32[:, j - 1, half(h)], in_=result[h][:, j - 1, :])
+                store_ready(0, 2)
+                for h in range(HALVES):
+                    nc.scalar.copy(out=o_bf[:, half(h), 0:2], in_=result[h][:, 0:2, :].rearrange("p j q -> p q j"))
+            if j == 3:
+                store_ready(2, 3)
         nc.sync.dma_start(out=out_dealt[:, 0 : PACK - 1, :], in_=o_f32[:, 0 : PACK - 1, :])
         scale_values(PACK - 1)
         quantise_values(PACK - 1)
         multiply(PACK - 1)
 
-        nc.vector.tensor_copy(out=o_bf[:, half(0), :], in_=result[0][:].rearrange("p j q -> p q j"))
-        nc.scalar.copy(out=o_bf[:, half(1), :], in_=result[1][:].rearrange("p j q -> p q j"))
+        nc.vector.tensor_copy(out=o_bf[:, half(0), 2:4], in_=result[0][:, 2:4, :].rearrange("p j q -> p q j"))
+        nc.scalar.copy(out=o_bf[:, half(1), 2:4], in_=result[1][:, 2:4, :].rearrange("p j q -> p q j"))
         for h in (1, 0):
             nc.scalar.copy(out=o_f32[:, PACK - 1, half(h)], in_=result[h][:, PACK - 1, :])
         for h in (1, 0):

@@ -22,6 +22,7 @@ PACK = 4
 HALVES = Q // P
 LIST_COLS = I // 16
 POOL_BYTES = 4 * T
+RUN = 8
 
 
 def tile_attend_keyhere_valuethere_pl_kernel(tc, query, keys_words, keys_scales, size, vsc, vals, svals, offs, offs2, out_0, out_1, out_2):
@@ -34,13 +35,14 @@ def tile_attend_keyhere_valuethere_pl_kernel(tc, query, keys_words, keys_scales,
         nc.vector.memset(key_bytes[:].bitcast(I32), 0)
         ident = keep.tile([P, P], F32, name="ident")
         make_identity(nc, ident[:])
+        factor_rows = keep.tile([P, P], F32, name="factor_rows")
+        nc.gpsimd.memset(factor_rows[:], 0.0)
 
         key_words = keep.tile([P, T], U16, name="key_words")
         list1 = keep.tile([P, LIST_COLS], U16, name="list1")
         list2 = keep.tile([P, LIST_COLS], U16, name="list2")
         q_raw = keep.tile([P, PACK, Q], F32, name="q_raw")
-        size_t = keep.tile([P, PACK], F32, name="size_t")
-        vsc_t = keep.tile([P, PACK], F32, name="vsc_t")
+        factors = keep.tile([P, 2 * PACK], F32, name="factors")
         tokens = ctx.enter_context(tc.tile_pool(name="tokens", bufs=1))
         s_at = [2 * j * POOL_BYTES for j in range(PACK)]
         v_at = [(2 * j + 1) * POOL_BYTES for j in range(PACK)]
@@ -51,14 +53,14 @@ def tile_attend_keyhere_valuethere_pl_kernel(tc, query, keys_words, keys_scales,
 
         nc.sync.dma_start(out=key_words[:].bitcast(I32), in_=keys_words[0].bitcast(I32))
         nc.sync.dma_start(list1[:], offs)
-        for g in range(4):
-            nc.sync.dma_start(out=key_bytes[32 * g : 32 * g + 4, :].bitcast(I32), in_=keys_scales[0, 4 * g : 4 * g + 4, :].bitcast(I32))
+        for r in range(4):
+            nc.sync.dma_start(out=key_bytes[r:P:32, :].bitcast(I32), in_=keys_scales[0, r:16:4, :].bitcast(I32))
         nc.sync.dma_start(out=q_raw[:], in_=query.rearrange("(p j) q -> p j q", j=PACK))
         nc.sync.dma_start(out=s_pool[0][:], in_=svals_dealt[:, 0, :])
         nc.sync.dma_start(list2[:], offs2)
         nc.sync.dma_start(out=v_pool[0][:], in_=vals_dealt[:, 0, :])
-        nc.sync.dma_start(out=vsc_t[:], in_=vsc.rearrange("(p t) o -> p (t o)", t=PACK))
-        nc.sync.dma_start(out=size_t[:], in_=size.rearrange("o (p t) -> p (o t)", t=PACK))
+        nc.sync.dma_start(out=factor_rows[0:PACK, :].rearrange("t (g r) -> t g r", r=RUN), in_=vsc.rearrange("(g t r) o -> t g (r o)", t=PACK, r=RUN))
+        nc.sync.dma_start(out=factor_rows[PACK : 2 * PACK, :].rearrange("t (g r) -> t g r", r=RUN), in_=size.rearrange("o (g t r) -> t (o g) r", t=PACK, r=RUN))
         for j in range(1, PACK):
             nc.sync.dma_start(out=s_pool[j][:], in_=svals_dealt[:, j, :])
             nc.sync.dma_start(out=v_pool[j][:], in_=vals_dealt[:, j, :])
@@ -88,6 +90,12 @@ def tile_attend_keyhere_valuethere_pl_kernel(tc, query, keys_words, keys_scales,
         def half(h):
             return slice(h * P, (h + 1) * P)
 
+        def by_place(dealt):
+            return dealt.rearrange("p t (g r) -> p g t r", r=RUN)
+
+        def by_slot(listed):
+            return listed.rearrange("p (g t r) -> p g t r", t=PACK, r=RUN)
+
         def quantise(codes, scales, source):
             nc.vector.quantize_mx(out=codes.bitcast(FP8X4), scales=scales, in_=source.rearrange("p c t -> p (c t)"))
 
@@ -96,20 +104,20 @@ def tile_attend_keyhere_valuethere_pl_kernel(tc, query, keys_words, keys_scales,
             s_got = keep.tile([P, I], F32, name="s_got%d" % j, align_bytes=64)
             s_tanh = keep.tile([P, PACK, P], F32, name="s_tanh%d" % j)
             nc.vector.tensor_copy(s_got[:], s_pool[j][:].indirect(list1[:]))
-            nc.scalar.activation(out=s_tanh[:].rearrange("p t s -> p s t"), in_=s_got[:].rearrange("p (s t) -> p s t", t=PACK), func=ACT.Tanh)
+            nc.scalar.activation(out=by_place(s_tanh[:]), in_=by_slot(s_got[:]), func=ACT.Tanh)
             for t in range(PACK):
                 nc.tensor.matmul(v_sum[j][:, t, :], lhsT=s_tanh[:, t, :], rhs=ident[:], is_transpose=True, start=(t == 0), stop=False)
 
         def gather_vals(j):
             v_got = keep.tile([P, PACK, P], F32, name="v_got%d" % j)
-            nc.vector.tensor_copy(v_got[:].bitcast(U32).rearrange("p t s -> p s t"), v_pool[j][:].bitcast(U32).indirect(list2[:]))
+            nc.vector.tensor_copy(by_place(v_got[:].bitcast(U32)), v_pool[j][:].bitcast(U32).indirect(list2[:]))
             for t in range(PACK):
                 nc.tensor.matmul(v_sum[j][:, t, :], lhsT=v_got[:, t, :], rhs=ident[:], is_transpose=True, start=False, stop=(t == PACK - 1))
 
         def scale_values(j):
             v_bf[j] = tokens.tile([P, P, PACK], BF16, name="v_bf%d" % j, offset=s_at[(j + 1) % PACK] + 1024, align_bytes=64)
             nc.vector.tensor_tensor(out=v_bf[j][:], in0=v_sum[j][:].rearrange("p t e -> p e t"),
-                                    in1=vsc_t[:].unsqueeze(1).broadcast_to([P, P, PACK]), op=ALU.mult)
+                                    in1=factors[:, 0:PACK].unsqueeze(1).broadcast_to([P, P, PACK]), op=ALU.mult)
 
         def quantise_values(j):
             v_codes[j] = tokens.tile([P, P], U32, name="v_codes%d" % j, offset=v_at[(j + 1) % PACK] + 1024, align_bytes=64)
@@ -137,10 +145,12 @@ def tile_attend_keyhere_valuethere_pl_kernel(tc, query, keys_words, keys_scales,
         gather_svals(0)
         for h in range(HALVES):
             nc.vector.tensor_reduce(out=neg_max[:, h : h + 1], in_=score[h][:], axis=mybir.AxisListType.X, op=ALU.max, negate=True)
-            nc.scalar.activation(out=p_dealt[h][:].rearrange("p t s -> p s t"), in_=score[h][:].rearrange("p (s t) -> p s t", t=PACK),
+            nc.scalar.activation(out=by_place(p_dealt[h][:]), in_=by_slot(score[h][:]),
                                  func=ACT.Exp, bias=neg_max[:, h : h + 1], scale=1.0, accum_out=row_sum[:, h : h + 1])
         gather_vals(0)
         nc.vector.reciprocal(out=inv_sum[:], in_=row_sum[:])
+        nc.tensor.transpose(result[0][:, 0, :], factor_rows[:], ident[:])
+        nc.scalar.copy(out=factors[:], in_=result[0][:, 0, 0 : 2 * PACK])
         for h in range(HALVES):
             nc.scalar.activation(out=p_norm[h][:], in_=p_dealt[h][:], func=ACT.Copy, scale=inv_sum[:, h : h + 1])
             for t in range(PACK):
@@ -151,7 +161,7 @@ def tile_attend_keyhere_valuethere_pl_kernel(tc, query, keys_words, keys_scales,
                 w_bf = keep.tile([P, Q, PACK], BF16, name="w_bf", tag="s_got1", align_bytes=64)
                 for h in range(HALVES):
                     for t in range(PACK):
-                        nc.scalar.activation(out=w_bf[:, half(h), t], in_=p_turned[h][:, t, :], func=ACT.Copy, scale=size_t[:, t : t + 1])
+                        nc.scalar.activation(out=w_bf[:, half(h), t], in_=p_turned[h][:, t, :], func=ACT.Copy, scale=factors[:, PACK + t : PACK + t + 1])
             scale_values(j - 1)
             gather_vals(j)
             quantise_values(j - 1)

from contextlib import ExitStack

import concourse.mybir as mybir
from concourse.masks import make_identity

D, T, I, Q, E = 512, 2048, 512, 256, 512
FLOPS = 2 * Q * I * D + 2 * E * I * Q

F32 = mybir.dt.float32
BF16 = mybir.dt.bfloat16
I32 = mybir.dt.int32
U32 = mybir.dt.uint32
U16 = mybir.dt.uint16
U8 = mybir.dt.uint8
FP8X4 = mybir.dt.float8_e4m3fn_x4
FP4X4 = mybir.dt.float4_e2m1fn_x4
ACT = mybir.ActivationFunctionType
ALU = mybir.AluOpType

P = 128
PACK = 4
HALVES = Q // P
LIST_COLS = I // 16
POOL_BYTES = 4 * T
RUN = 8


def tile_attend_keyhere_valuethere_pl_kernel(tc, query, keys_words, keys_scales, size, vsc, vals, svals, offs, offs2, out_0, out_1, out_2):
    nc = tc.nc
    with ExitStack() as ctx:
        keep = ctx.enter_context(tc.tile_pool(name="keep", bufs=1))
        psum = ctx.enter_context(tc.psum_pool(name="psum", bufs=1))

        key_bytes = keep.tile([P, T], U8, name="key_bytes")
        nc.vector.memset(key_bytes[:].bitcast(I32), 0)
        ident = keep.tile([P, P], F32, name="ident")
        make_identity(nc, ident[:])
        factor_rows = keep.tile([P, P], F32, name="factor_rows")
        nc.gpsimd.memset(factor_rows[:], 0.0)

        key_words = keep.tile([P, T], U16, name="key_words")
        list1 = keep.tile([P, LIST_COLS], U16, name="list1")
        list2 = keep.tile([P, LIST_COLS], U16, name="list2")
        q_raw = keep.tile([P, PACK, Q], F32, name="q_raw")
        factors = keep.tile([P, 2 * PACK], F32, name="factors")
        tokens = ctx.enter_context(tc.tile_pool(name="tokens", bufs=1))
        s_at = [2 * j * POOL_BYTES for j in range(PACK)]
        v_at = [(2 * j + 1) * POOL_BYTES for j in range(PACK)]
        s_pool = [tokens.tile([P, T], F32, name="s_pool%d" % j, offset=s_at[j], align_bytes=64) for j in range(PACK)]
        v_pool = [tokens.tile([P, T], F32, name="v_pool%d" % j, offset=v_at[j], align_bytes=64) for j in range(PACK)]
        vals_dealt = vals.rearrange("(p j) t -> p j t", j=PACK)
        svals_dealt = svals.rearrange("(p j) t -> p j t", j=PACK)

        nc.sync.dma_start(out=key_words[:].bitcast(I32), in_=keys_words[0].bitcast(I32))
        nc.sync.dma_start(list1[:], offs)
        for r in range(4):
            nc.sync.dma_start(out=key_bytes[r:P:32, :].bitcast(I32), in_=keys_scales[0, r:16:4, :].bitcast(I32))
        nc.sync.dma_start(out=q_raw[:], in_=query.rearrange("(p j) q -> p j q", j=PACK))
        nc.sync.dma_start(out=s_pool[0][:], in_=svals_dealt[:, 0, :])
        nc.sync.dma_start(list2[:], offs2)
        nc.sync.dma_start(out=v_pool[0][:], in_=vals_dealt[:, 0, :])
        nc.sync.dma_start(out=factor_rows[0:PACK, :].rearrange("t (g r) -> t g r", r=RUN), in_=vsc.rearrange("(g t r) o -> t g (r o)", t=PACK, r=RUN))
        nc.sync.dma_start(out=factor_rows[PACK : 2 * PACK, :].rearrange("t (g r) -> t g r", r=RUN), in_=size.rearrange("o (g t r) -> t (o g) r", t=PACK, r=RUN))
        for j in range(1, PACK):
            nc.sync.dma_start(out=s_pool[j][:], in_=svals_dealt[:, j, :])
            nc.sync.dma_start(out=v_pool[j][:], in_=vals_dealt[:, j, :])

        k_codes = keep.tile([P, I], U16, name="k_codes", align_bytes=64)
        k_scales = keep.tile([P, I], U8, name="k_scales", align_bytes=64)
        q_bf = keep.tile([P, Q, PACK], BF16, name="q_bf", tag="s_got0", align_bytes=64)
        q_codes = keep.tile([P, Q], U32, name="q_codes", align_bytes=64)
        q_scales = keep.tile([P, Q], U8, name="q_scales", align_bytes=64)
        w_codes = tokens.tile([P, Q], U32, name="w_codes", offset=v_at[2], align_bytes=64)
        w_scales = keep.tile([P, Q], U8, name="w_scales", align_bytes=64)
        neg_max = tokens.tile([P, HALVES], F32, name="neg_max", offset=s_at[0], align_bytes=64)
        row_sum = keep.tile([P, HALVES], F32, name="row_sum")
        inv_sum = tokens.tile([P, HALVES], F32, name="inv_sum", offset=v_at[0], align_bytes=64)
        p_dealt = [keep.tile([P, PACK, P], F32, name="p_dealt%d" % h) for h in range(HALVES)]
        p_norm = [keep.tile([P, PACK, P], F32, name="p_norm%d" % h) for h in range(HALVES)]
        score = [psum.tile([P, I], F32, name="score%d" % h) for h in range(HALVES)]
        p_turned = [psum.tile([P, PACK, P], F32, name="p_turned%d" % h) for h in range(HALVES)]
        result = [psum.tile([P, PACK, P], F32, name="result%d" % h) for h in range(HALVES)]
        o_f32 = keep.tile([P, PACK, Q], F32, name="o_f32")
        o_bf = keep.tile([P, Q, PACK], BF16, name="o_bf", align_bytes=64)
        o_codes = keep.tile([P, Q], U32, name="o_codes", align_bytes=64)
        o_scales = keep.tile([P, Q], U8, name="o_scales", align_bytes=64)
        out_dealt = out_0.rearrange("(p j) q -> p j q", j=PACK)
        v_sum, v_bf, v_codes, v_scales = {}, {}, {}, {}

        def half(h):
            return slice(h * P, (h + 1) * P)

        def by_place(dealt):
            return dealt.rearrange("p t (g r) -> p g t r", r=RUN)

        def by_slot(listed):
            return listed.rearrange("p (g t r) -> p g t r", t=PACK, r=RUN)

        def quantise(codes, scales, source):
            nc.vector.quantize_mx(out=codes.bitcast(FP8X4), scales=scales, in_=source.rearrange("p c t -> p (c t)"))

        def gather_svals(j):
            v_sum[j] = psum.tile([P, PACK, P], F32, name="v_sum", bufs=2)
            s_got = keep.tile([P, I], F32, name="s_got%d" % j, align_bytes=64)
            s_tanh = keep.tile([P, PACK, P], F32, name="s_tanh%d" % j)
            nc.vector.tensor_copy(s_got[:], s_pool[j][:].indirect(list1[:]))
            nc.scalar.activation(out=by_place(s_tanh[:]), in_=by_slot(s_got[:]), func=ACT.Tanh)
            for t in range(PACK):
                nc.tensor.matmul(v_sum[j][:, t, :], lhsT=s_tanh[:, t, :], rhs=ident[:], is_transpose=True, start=(t == 0), stop=False)

        def gather_vals(j):
            v_got = keep.tile([P, PACK, P], F32, name="v_got%d" % j)
            nc.vector.tensor_copy(by_place(v_got[:].bitcast(U32)), v_pool[j][:].bitcast(U32).indirect(list2[:]))
            for t in range(PACK):
                nc.tensor.matmul(v_sum[j][:, t, :], lhsT=v_got[:, t, :], rhs=ident[:], is_transpose=True, start=False, stop=(t == PACK - 1))

        def scale_values(j):
            v_bf[j] = tokens.tile([P, P, PACK], BF16, name="v_bf%d" % j, offset=s_at[(j + 1) % PACK] + 1024, align_bytes=64)
            nc.vector.tensor_tensor(out=v_bf[j][:], in0=v_sum[j][:].rearrange("p t e -> p e t"),
                                    in1=factors[:, 0:PACK].unsqueeze(1).broadcast_to([P, P, PACK]), op=ALU.mult)

        def quantise_values(j):
            v_codes[j] = tokens.tile([P, P], U32, name="v_codes%d" % j, offset=v_at[(j + 1) % PACK] + 1024, align_bytes=64)
            v_scales[j] = keep.tile([P, P], U8, name="v_scales%d" % j, align_bytes=64)
            quantise(v_codes[j][:], v_scales[j][:], v_bf[j][:])

        def multiply(j):
            for h in range(HALVES):
                nc.tensor.matmul_mx(out=result[h][:, j, :], lhsT=v_codes[j][:].bitcast(FP8X4), lhsT_scale=v_scales[j][:],
                                    rhs=w_codes[:, half(h)].bitcast(FP8X4), rhs_scale=w_scales[:, half(h)], start=True, stop=True)

        def store_ready(first, last):
            for j in range(first, last):
                multiply(j)
            for h in range(HALVES):
                nc.scalar.copy(out=o_f32[:, first:last, half(h)], in_=result[h][:, first:last, :])

        nc.vector.tensor_copy(k_codes[:], key_words[:].indirect(list1[:]))
        nc.vector.tensor_copy(k_scales[:], key_bytes[:].indirect(list1[:]))
        nc.scalar.copy(out=q_bf[:], in_=q_raw[:].rearrange("p j q -> p q j"))
        quantise(q_codes[:], q_scales[:], q_bf[:])
        for h in range(HALVES):
            nc.tensor.matmul_mx(out=score[h][:], lhsT=q_codes[:, half(h)].bitcast(FP8X4), lhsT_scale=q_scales[:, half(h)],
                                rhs=k_codes[:].bitcast(FP4X4), rhs_scale=k_scales[:], start=True, stop=True)
        gather_svals(0)
        for h in range(HALVES):
            nc.vector.tensor_reduce(out=neg_max[:, h : h + 1], in_=score[h][:], axis=mybir.AxisListType.X, op=ALU.max, negate=True)
            nc.scalar.activation(out=by_place(p_dealt[h][:]), in_=by_slot(score[h][:]),
                                 func=ACT.Exp, bias=neg_max[:, h : h + 1], scale=1.0, accum_out=row_sum[:, h : h + 1])
        gather_vals(0)
        nc.vector.reciprocal(out=inv_sum[:], in_=row_sum[:])
        nc.tensor.transpose(result[0][:, 0, :], factor_rows[:], ident[:])
        nc.scalar.copy(out=factors[:], in_=result[0][:, 0, 0 : 2 * PACK])
        for h in range(HALVES):
            nc.scalar.activation(out=p_norm[h][:], in_=p_dealt[h][:], func=ACT.Copy, scale=inv_sum[:, h : h + 1])
            for t in range(PACK):
                nc.tensor.transpose(p_turned[h][:, t, :], p_norm[h][:, t, :], ident[:])
        for j in range(1, PACK):
            gather_svals(j)
            if j == 1:
                w_bf = keep.tile([P, Q, PACK], BF16, name="w_bf", tag="s_got1", align_bytes=64)
                for h in range(HALVES):
                    for t in range(PACK):
                        nc.scalar.activation(out=w_bf[:, half(h), t], in_=p_turned[h][:, t, :], func=ACT.Copy, scale=factors[:, PACK + t : PACK + t + 1])
            scale_values(j - 1)
            gather_vals(j)
            quantise_values(j - 1)
            if j == 2:
                quantise(w_codes[:], w_scales[:], w_bf[:])
                store_ready(0, 2)
                for h in range(HALVES):
                    nc.scalar.copy(out=o_bf[:, half(h), 0:2], in_=result[h][:, 0:2, :].rearrange("p j q -> p q j"))
            if j == 3:
                store_ready(2, 3)
        nc.sync.dma_start(out=out_dealt[:, 0 : PACK - 1, :], in_=o_f32[:, 0 : PACK - 1, :])
        scale_values(PACK - 1)
        quantise_values(PACK - 1)
        multiply(PACK - 1)

        nc.vector.tensor_copy(out=o_bf[:, half(0), 2:4], in_=result[0][:, 2:4, :].rearrange("p j q -> p q j"))
        nc.scalar.copy(out=o_bf[:, half(1), 2:4], in_=result[1][:, 2:4, :].rearrange("p j q -> p q j"))
        for h in (1, 0):
            nc.scalar.copy(out=o_f32[:, PACK - 1, half(h)], in_=result[h][:, PACK - 1, :])
        for h in (1, 0):
            quantise(o_codes[:, half(h)], o_scales[:, half(h)], o_bf[:, half(h), :])
        nc.scalar.dma_start(out=out_dealt[:, PACK - 1, :], in_=o_f32[:, PACK - 1, :])
        nc.sync.dma_start(out=out_1[0].rearrange("p q r -> p (q r)").bitcast(I32), in_=o_codes[:].bitcast(I32))
        for g in range(4):
            queue = nc.sync if g < 2 else nc.scalar
            queue.dma_start(out=out_2[0, 4 * g : 4 * g + 4, :].bitcast(I32), in_=o_scales[32 * g : 32 * g + 4, :].bitcast(I32))
